import numpy as np, ml_dtypes
CORES = [12,28,60,100,156,228]
N = 6
import mx_ref
BF = ml_dtypes.bfloat16
def entries(a):
    return np.ascontiguousarray(a.T).reshape(-1)
def table(e):
    return np.ascontiguousarray(np.reshape(e, (-1, 16)).T).astype(np.int32)
def cols(t, e):
    v = np.concatenate([t.reshape(128, -1, 4), np.zeros((128, 1, 4), BF)], axis=1)
    return np.ascontiguousarray(v[:, e]).reshape(128, -1)
def f(rng, *shape):
    return mx_ref.flush((rng.standard_normal(shape, dtype=np.float32) * np.exp2(rng.integers(-2, 3, shape[:-1] + (1,)))).astype(BF))
def wide(rng, *shape, cols=0):
    v = rng.standard_normal(shape, dtype=np.float32) * np.exp2(rng.integers(-12, 13, shape)).astype(np.float32)
    if cols: v *= np.repeat(np.exp2(rng.integers(-cols, cols + 1, shape[:-2] + (1, shape[-1] // 4))) * (rng.random(shape[:-2] + (1, shape[-1] // 4)) > 0.0625), 4, axis=-1).astype(np.float32)
    return mx_ref.flush(v.astype(BF))
T, S, CAPP = 512, 192, 48
def lists(rng, most=None, own=False, share=False, edge=False):
    o, c, m = [], [], []
    for r in range(N):
        n = np.zeros(N, int)
        if own: n[r] = CAPP
        if most is not None:
            for q in rng.permutation(N)[:most]: n[q] = CAPP
            n = np.minimum(n, np.maximum(0, S - (np.cumsum(n) - n)))
        while n.sum() < S:
            q = rng.integers(0, N)
            if n[q] < CAPP: n[q] += 1
        slots = np.full(N * CAPP, -1); used = []
        for q in range(N):
            k = q * CAPP + rng.permutation(CAPP)[:n[q]]; used += list(k)
            slots[k] = rng.integers(0, T) if share else rng.choice([0, T - 1], n[q]) if edge else rng.integers(0, T, n[q])
        o.append(table(rng.choice([0, T - 1], S) if edge else rng.integers(0, T, S))); c.append(table(slots)); m.append(table(rng.permutation(used)))
    return {"own": np.stack(o), "want": np.stack(c), "slot": np.stack(m)}
def setup_inputs(rng):
    return {"x": f(rng, N, 128, 4 * T), "w": f(rng, N, 128, 512), **lists(rng)}
def setup_inputs_edge(rng):
    return {**setup_inputs(rng), **lists(rng, edge=True)}
def setup_inputs_full(rng):
    return {**setup_inputs(rng), **lists(rng, most=S // CAPP)}
def setup_inputs_self(rng):
    return {**setup_inputs(rng), **lists(rng, own=True)}
def setup_inputs_share(rng):
    return {**setup_inputs(rng), **lists(rng, share=True)}
def setup_inputs_spread(rng):
    d = setup_inputs(rng); d["x"] = wide(rng, N, 128, 4 * T, cols=8); return d
def check_inputs(d):
    b = []
    for r in range(N):
        o, c, m = entries(d["own"][r]), entries(d["want"][r]), entries(d["slot"][r])
        if o.min() < 0 or o.max() >= T: b.append("own")
        if c.min() < -1 or c.max() >= T: b.append("want")
        if m.min() < 0 or m.max() >= N * CAPP or len(set(m.tolist())) != S or (c[m] < 0).any() or (c >= 0).sum() != S: b.append("slot")
    return b
def decode(q):
    out = np.zeros(q[0].shape, np.float32)
    for b in range(4):
        e = np.zeros((128, 128, 4), np.float32); e[np.arange(128), np.arange(128), b] = 1
        out[:, b::4] = mx_ref.matmul(mx_ref.quantize(e.reshape(128, 512).astype(BF)), q)
    return out
def reference(x, w, own, want, slot):
    M = []
    for r in range(N):
        c = entries(want[r])
        arrived = np.concatenate([decode(mx_ref.quantize(cols(x[q], c[q * CAPP:(q + 1) * CAPP]))) for q in range(N)], axis=1)
        far = arrived.reshape(128, -1, 4)[:, entries(slot[r])].reshape(128, -1)
        M.append(mx_ref.quantize(((cols(x[r], entries(own[r])).astype(np.float32) + far) * np.float32(0.5)).astype(BF)))
    y = np.zeros((N, 128, 3 * S), np.float32)
    for r in range(N):
        for i in range(3): y[r][:, S * i:S * i + S] = mx_ref.matmul(mx_ref.quantize(w[r]), M[(r - 1 + i) % N])
    return {"y": y}

from concourse.bass import DstId, RemoteDMATransfer
from concourse.mybir import dt, AluOpType, ActivationFunctionType

N, T_COLS, S, CAP = 6, 512, 192, 48
K = CAP // 16
W4 = 4 * T_COLS
F_W = N * CAP

X4, U8 = "float8_e4m3fn_x4", "uint8"
SCRATCH = {
    "xs": ("sbuf", [128, W4], "bfloat16"),
    "wt": ("sbuf", [128, 512], "bfloat16"),
    "wl": ("sbuf", [128, K * N], "int32"),
    "ol": ("sbuf", [128, S // 16], "int32"),
    "sl": ("sbuf", [128, S // 16], "int32"),
    "wu": ("sbuf", [128, K * N], "uint16"),
    "su": ("sbuf", [128, 4], "uint16"),
    "ou": ("sbuf", [128, S // 16], "uint16"),
    "so": ("sbuf", [128, S // 16], "uint16"),
    "ta": ("sbuf", [128, S // 16], "int32"),
    "tb": ("sbuf", [128, S // 16], "int32"),
    "tc": ("sbuf", [128, S // 16], "int32"),
    "td": ("sbuf", [128, S // 16], "int32"),
    "te": ("sbuf", [128, S // 16], "int32"),
    "tf": ("sbuf", [128, S // 16], "int32"),
    "li": ("sbuf", [128, 12], "uint16"),
    "lj": ("sbuf", [128, 12], "uint16"),
    "half": ("sbuf", [128, 128], "bfloat16"),
    "idt": ("sbuf", [128, 128], "bfloat16"),
    "e4": ("sbuf", [128, 2048], "bfloat16"),
    "qe": ("sbuf", [128, 512], X4),
    "qes": ("sbuf", [128, 512], U8),
    "wq": ("sbuf", [128, 128], X4),
    "wqs": ("sbuf", [128, 128], U8),
    "ga": ("sbuf", [128, 4 * 144], "bfloat16"),
    "gx": ("sbuf", [128, 4 * 192], "bfloat16"),
    "ac": ("sbuf", [128, 384], X4),
    "acs": ("sbuf", [128, 384], U8),
    "qx": ("sbuf", [128, 192], X4),
    "qxs": ("sbuf", [128, 192], U8),
    "oh": ("sbuf", [128, 4 * S], "bfloat16"),
    "ft": ("sbuf", [128, 4 * F_W], "bfloat16"),
    "mt": ("sbuf", [128, 4 * S], "bfloat16"),
    "qm": ("sbuf", [128, S], X4),
    "qms": ("sbuf", [128, S], U8),
    "ml": ("sbuf", [128, S], X4),
    "mls": ("sbuf", [128, S], U8),
    "mr": ("sbuf", [128, S], X4),
    "mrs": ("sbuf", [128, S], U8),
    "yb": ("sbuf", [128, 3 * S], "float32"),
    "rl": ("sbuf", [128, K * N], "uint16"),
    "rc": ("sbuf", [128, 2 * CAP], X4),
    "rcs": ("sbuf", [128, 2 * CAP], U8),
    "rm": ("sbuf", [128, S], X4),
    "rms": ("sbuf", [128, S], U8),
    "pe": ("psum", [128, 2048], "float32"),
    "pl": ("psum", [128, 2048], "float32"),
}
CODES = {k for k, v in SCRATCH.items() if v[2] == X4}
ARRIVALS = ["a_li", "a_lj", "a_ce", "a_cl", "a_ml", "a_mr", "r_l", "r_c", "r_cs", "r_m", "r_ms"]
EVENTS = (["ldw", "ldx", "ldo", "lds", "ldwt", "half", "e0", "pad", "idt", "wu", "su", "ou", "e1", "qe", "gs", "ge", "qearly",
           "gl", "qlate", "oh", "s1", "s2", "s3", "s4", "s5", "wq", "fe", "ma", "mq", "yst", "sent"]
          + ["me%d" % b for b in range(4)] + ["mlt%d" % b for b in range(4)] + ["fl%d" % b for b in range(4)]
          + ["y%d" % i for i in range(3)] + ["yc%d" % i for i in range(3)])
SEMAPHORES = ARRIVALS + EVENTS


def deal(engines, k, back=False):
    n = len(engines)
    sizes = [n // 2, n // 4, n // 4] if k == 3 else [n // k] * k
    if back:
        sizes = sizes[::-1]
    out, a = [], 0
    for s in sizes:
        out.append(engines[a:a + s])
        a += s
    return out


def groups(cores, topo):
    direct = [[q for q in range(N) if q != r and topo.may_write(cores[r], cores[q])] for r in range(N)]
    cross = [[q for q in range(N) if q != r and q not in direct[r]] for r in range(N)]
    return direct, cross


def layout(r, direct, cross):
    A, X = ("ga", "ac", "acs"), ("gx", "qx", "qxs")
    ne, nl = CAP * len(direct[r]), CAP * len(cross[r])
    if ne >= 128:
        na, nx, pad = nl + CAP, ne, 0
        early, late, me = X + (0,), A + (0,), nl
    else:
        na, nx = 128, nl
        pad = na - CAP - ne
        early, late, me = A + (pad,), X + (0,), pad + ne
    return {"na": na, "nx": nx, "pad": pad, "early": early, "late": late, "self": me, "ein": na, "lin": na + ne,
            "ne": ne, "nl": nl, "early_is_x": ne >= 128}


def make_plan(cores, topo):
    direct, cross = groups(cores, topo)
    lay = [layout(r, direct, cross) for r in range(N)]
    calls, due = {}, {}

    def call(core, tag, trs):
        calls.setdefault(core, []).append((tag, trs))
        for to, eng, src, dst, sem in trs:
            due[(to, sem)] = due.get((to, sem), 0) + len(eng)

    for r in range(N):
        c, L = cores[r], lay[r]
        D, X = direct[r], cross[r]
        ports = [p for p in topo.cores_of(c) if p != c and topo.may_write(p, cores[X[0]])]
        near = [p for p in ports if topo.die(p) == topo.die(c)]
        far = [p for p in ports if topo.die(p) != topo.die(c)]
        rel = [near[0], far[0], far[1], near[1]][:len(X)]
        out = topo.engines(c, cores[D[0]])
        every = topo.engines(c, rel[0])
        inside = [e for e in every if e not in out]
        four = len(rel) == 4

        def away(p):
            return topo.engines(p, cores[X[0]])

        sh = deal(inside, len(rel))
        call(c, "list", [(p, sh[i], ("wu", 0, K * N), ("rl", 0, K * N), "r_l") for i, p in enumerate(rel)])
        for i, p in enumerate(rel):
            q = X[i]
            j = cross[q].index(r)
            call(p, "r_l", [(cores[q], away(p), ("rl", K * q, K * q + K), ("lj", K * j, K * j + K), "a_lj")])
        sh = deal(out, len(D))
        call(c, "list", [(cores[q], sh[i], ("wu", K * q, K * q + K),
                          ("li", K * direct[q].index(r), K * direct[q].index(r) + K), "a_li") for i, q in enumerate(D)])

        def place(buf, q, late):
            a = lay[q]["lin"] + CAP * cross[q].index(r) if late else lay[q]["ein"] + CAP * direct[q].index(r)
            return (buf, a, a + CAP)

        for buf, land, back in ((L["early"][1], "ac", False), (L["early"][2], "acs", True)):
            sh = deal(out, len(D), back)
            a = L["early"][3]
            call(c, "early", [(cores[q], sh[i], (buf, a + CAP * i, a + CAP * i + CAP), place(land, q, False), "a_ce")
                              for i, q in enumerate(D)])
        a = L["late"][3]
        if four:
            parts = [(X[:2], 0, rel[0], rel[2]), (X[2:], 2 * CAP, rel[1], rel[3])]
        else:
            flip = (sorted(D + [r]).index(r)) % 2
            parts = [(X, 0, rel[flip], rel[1 - flip])]
        ec, es = deal(inside, len(parts)), deal(out if four else inside, len(parts))
        call(c, "late", [(p[2], ec[i], (L["late"][1], a + p[1], a + p[1] + 2 * CAP), ("rc", 0, 2 * CAP), "r_c")
                         for i, p in enumerate(parts)])
        call(c, "late", [(p[3], es[i], (L["late"][2], a + p[1], a + p[1] + 2 * CAP), ("rcs", 0, 2 * CAP), "r_cs")
                         for i, p in enumerate(parts)])
        for qs, _, pc, ps in parts:
            for p, tag, src, land in ((pc, "r_c", "rc", "ac"), (ps, "r_cs", "rcs", "acs")):
                sh = deal(away(p), len(qs))
                call(p, tag, [(cores[q], sh[i], (src, CAP * i, CAP * i + CAP), place(land, q, True), "a_cl")
                              for i, q in enumerate(qs)])

        ways = [((r + 1) % N, "ml", "mls", "a_ml", 0), ((r - 1) % N, "mr", "mrs", "a_mr", 1)]
        over = [w for w in ways if w[0] in X]
        here = [w for w in ways if w[0] in D]
        if over:
            sh = deal(every, len(over))
            for b in ((0, 1) if four else (1, 0)):
                s, l, sem = (("qm", "rm", "r_m"), ("qms", "rms", "r_ms"))[b]
                via = [rel[w[4] + (2 * b if four else 0)] for w in over]
                call(c, "m", [(p, sh[i], (s, 0, S), (l, 0, S), sem) for i, p in enumerate(via)])
                for p, w in zip(via, over):
                    call(p, sem, [(cores[w[0]], away(p), (l, 0, S), (w[1 + b], 0, S), w[3])])
        if here:
            sh = deal(out, len(here))
            for b in (0, 1):
                call(c, "m", [(cores[w[0]], sh[i], (("qm", "qms")[b], 0, S), (w[1 + b], 0, S), w[3])
                              for i, w in enumerate(here)])
    return direct, cross, lay, calls, due


def rank_program(g, core, T, topo):
    direct, cross, lay, calls, due = make_plan(T.cores, topo)
    mine = calls.get(core)
    if mine is None:
        return
    count, waited = {}, set()

    def view(v):
        a = T[v[0]][:, v[1]:v[2]]
        return a.bitcast(dt.uint8) if v[0] in CODES else a

    def inc(ins, name, n=1):
        ins.then_inc(T.sem[name], n)
        count[name] = count.get(name, 0) + n

    def wait(q, *names):
        for name in names:
            q.wait_ge(T.sem[name], due[(core, name)] if (core, name) in due else count[name])
            waited.add(name)

    def send(trs):
        out = []
        for to, eng, src, dst, sem in trs:
            rid, pid = topo.addr(to, core)
            out.append(RemoteDMATransfer(dst_ids=[DstId(rid=rid, pnc=pid)], dma_engine_mask=sum(1 << e for e in eng),
                                         remote_sem=T.sem[sem], src=view(src), dst=view(dst)))
            count["sent"] = count.get("sent", 0) + len(eng)
        g.remote_dma_fused(out, local_sem=T.sem["sent"])

    def send_all(tag):
        for t, trs in mine:
            if t == tag:
                send(trs)

    r = T.rank_of(core)
    if r is None:
        for tag, trs in mine:
            wait(g, tag)
            send(trs)
        wait(g, "sent")
        return

    vec, act, ten, syn = g.vector, g.scalar, g.tensor, g.sync
    L, D, X = lay[r], direct[r], cross[r]
    copy = ActivationFunctionType.Copy
    add, mult = AluOpType.add, AluOpType.mult

    for k in range(8):
        inc((syn if k < 4 else act).dma_start(T["wl"][16 * k:16 * k + 16, :], T.want[:]), "ldw", 16)
    inc(syn.dma_start(T["xs"][:], T.x[:]), "ldx", 16)
    for k in range(8):
        inc(act.dma_start(T["ol"][16 * k:16 * k + 16, :], T.own[:]), "ldo", 16)
    for k in range(8):
        inc(syn.dma_start(T["sl"][16 * k:16 * k + 16, :], T.slot[:]), "lds", 16)
    inc(syn.dma_start(T["wt"][:], T.w[:]), "ldwt", 16)

    inc(vec.memset(T["half"][:], 0.5), "half")
    if L["pad"]:
        inc(vec.memset(T["ga"][:, 0:4 * L["pad"]], 0.0), "pad")
    wait(g, "half")
    inc(g.affine_select(T["idt"][:], T["half"][:], [[-1, 128]], AluOpType.is_equal, 0.0, 0, 1), "idt")
    wait(vec, "ldw")
    inc(vec.tensor_scalar(T["wu"][:], T["wl"][:], 0.0, 4.0, AluOpType.max, mult), "wu")
    wait(g, "wu")
    send_all("list")
    inc(vec.tensor_scalar(T["su"][:, 0:K], T["wl"][:, K * r:K * r + K], 0.0, 4.0, AluOpType.max, mult), "su")
    inc(vec.memset(T["e4"][:], 0.0), "e0")
    wait(vec, "e0", "idt")
    for b in range(4):
        inc(vec.tensor_copy(T["e4"][:, 512 * b + b:512 * b + 512:4], T["idt"][:]), "e1")
    wait(vec, "e1")
    inc(vec.quantize_mx(T["qe"][:], T["qes"][:], T["e4"][:]), "qe")
    wait(vec, "ldo")
    inc(vec.tensor_scalar(T["ou"][:], T["ol"][:], 4.0, None, mult), "ou")

    def gather(q, tile, a, n, off, t, name):
        dst = T[tile][:, 4 * a + t:4 * (a + n):4]
        src = T["xs"][:, t:W4].indirect(T[off][:, 0:n // 16])
        inc(q.tensor_copy(dst, src) if q is vec else q.activation(dst, src, copy), name)

    wait(act, "su", "ldx")
    for t in range(4):
        gather(act, "ga", L["self"], CAP, "su", t, "gs")
    wait(vec, "ldx")
    for sem, off, part, n, ev, qev in (("a_li", "li", L["early"], L["ne"], "ge", "qearly"),
                                       ("a_lj", "lj", L["late"], L["nl"], "gl", "qlate")):
        wait(vec, sem)
        wait(act, sem)
        for t in (0, 1):
            gather(vec, part[0], part[3], n, off, t, ev)
            gather(act, part[0], part[3], n, off, t + 2, ev)
        wait(vec, ev)
        if part[0] == "ga":
            wait(vec, "gs")
            if L["pad"]:
                wait(vec, "pad")
        w = L["na"] if part[0] == "ga" else L["nx"]
        inc(vec.quantize_mx(T[part[1]][:, 0:w], T[part[2]][:, 0:w], T[part[0]][:, 0:4 * w]), qev)
        wait(g, qev)
        send_all("early" if ev == "ge" else "late")

    wait(act, "ou")
    for t in range(4):
        inc(act.activation(T["oh"][:, S * t:S * t + S], T["xs"][:, t:W4].indirect(T["ou"][:, 0:S // 16]), copy, scale=0.5), "oh")
    order = sorted(D + [r]) if L["early_is_x"] else X
    order = order + [q for q in range(N) if q not in order]
    pos = [order.index(q) for q in range(N)]
    steps = [(j, pos[j] - pos[j - 1] - 1) for j in range(1, N) if pos[j] - pos[j - 1] != 1]
    wait(vec, "lds")
    terms = []
    for (j, d), tmp in zip(steps, ("ta", "tb", "tc")):
        inc(vec.tensor_scalar(T[tmp][:], T["sl"][:], float(CAP * j), float(CAP * d), AluOpType.is_ge, mult), "s1")
        terms.append(tmp)
    wait(vec, "ldwt")
    inc(vec.quantize_mx(T["wq"][:], T["wqs"][:], T["wt"][:]), "wq")
    wait(vec, "s1")
    acc = "sl"
    for tmp, to, ev in zip(terms, ("td", "te", "tf"), ("s2", "s3", "s4")):
        inc(vec.tensor_tensor(T[to][:], T[acc][:], T[tmp][:], add), ev)
        wait(vec, ev)
        acc = to
    inc(vec.tensor_copy(T["so"][:], T[acc][:]), "s5")

    lo, hi = min(L["self"], L["lin"] - 128), L["lin"]
    wait(ten, "qe", "qlate" if L["early_is_x"] else "qearly", "a_ce")
    for b in range(4):
        inc(ten.matmul_mx(T["pe"][:, 512 * b:512 * b + hi - lo], T["qe"][:, 128 * b:128 * b + 128], T["qes"][:, 128 * b:128 * b + 128],
                          T["ac"][:, lo:hi], T["acs"][:, lo:hi], True, True), "me%d" % b)
    runs = []
    for q, a in sorted([(r, L["self"])] + [(q, L["ein"] + CAP * i) for i, q in enumerate(D)], key=lambda v: pos[v[0]]):
        if runs and runs[-1][0] + runs[-1][2] == a - lo and runs[-1][1] + runs[-1][2] == CAP * pos[q]:
            runs[-1][2] += CAP
        else:
            runs.append([a - lo, CAP * pos[q], CAP])

    def unpack(q, ps, b, a, f, n, ev):
        dst, src = T["ft"][:, F_W * b + f:F_W * b + f + n], T[ps][:, 512 * b + a:512 * b + a + n]
        inc(q.tensor_copy(dst, src) if q is vec else q.activation(dst, src, copy), ev)

    for b in range(4):
        q = vec if b < 2 else act
        wait(q, "me%d" % b)
        for a, f, n in runs:
            unpack(q, "pe", b, a, f, n, "fe")

    end = L["lin"] + L["nl"]
    lo = min(L["lin"], end - 128)
    wait(ten, "a_cl")
    for b in range(4):
        inc(ten.matmul_mx(T["pl"][:, 512 * b:512 * b + end - lo], T["qe"][:, 128 * b:128 * b + 128], T["qes"][:, 128 * b:128 * b + 128],
                          T["ac"][:, lo:end], T["acs"][:, lo:end], True, True), "mlt%d" % b)
    for b in range(4):
        q = vec if b == 0 else act
        wait(q, "mlt%d" % b)
        unpack(q, "pl", b, L["lin"] - lo, CAP * pos[X[0]], L["nl"], "fl%d" % b)
    wait(vec, "fe", "s5", "oh")
    for b in range(4):
        wait(vec, "fl%d" % b)
        inc(vec.tensor_tensor(T["mt"][:, b:4 * S:4], T["ft"][:, F_W * b:F_W * b + F_W].indirect(T["so"][:, 0:S // 16]),
                              T["oh"][:, S * b:S * b + S], add), "ma")
    wait(vec, "ma")
    inc(vec.quantize_mx(T["qm"][:], T["qms"][:], T["mt"][:]), "mq")
    wait(g, "mq")
    send_all("m")

    sides = [(0, "ml", "mls", "a_ml", (r - 1) % N), (2, "mr", "mrs", "a_mr", (r + 1) % N)]
    sides.sort(key=lambda v: v[4] in X)
    wait(ten, "wq", "fe", "mq")
    for i, buf, pl, sem, _ in [(1, "qm", "qms", None, r)] + sides:
        if sem:
            wait(ten, sem)
        inc(ten.matmul_mx(T["pe"][:, 512 * i:512 * i + S], T["wq"][:], T["wqs"][:], T[buf][:], T[pl][:], True, True), "y%d" % i)
        q, dq = (act, act) if i == 2 else (vec, syn)
        wait(q, "y%d" % i)
        dst, src = T["yb"][:, S * i:S * i + S], T["pe"][:, 512 * i:512 * i + S]
        inc(q.tensor_copy(dst, src) if q is vec else q.activation(dst, src, copy), "yc%d" % i)
        wait(dq, "yc%d" % i)
        inc(dq.dma_start(T.y[:, S * i:S * i + S], dst), "yst", 16)
    wait(g, "yst", "sent")
    for name in count:
        if name not in waited:
            wait(g, name)
